import numpy as np
import ml_dtypes

BF16 = ml_dtypes.bfloat16


def bf(x):
    return np.asarray(x, np.float32).astype(BF16)


def f32(x):
    return np.asarray(x, np.float32)


def f64(x):
    return np.asarray(x).astype(np.float64)


def striped(idx):
    return np.tile(idx.reshape(-1, 16).T, (8, 1))


S, K, M, N, E, Q, O = 512, 128, 384, 256, 4, 64, 512


def gelu_tanh(v):
    return 0.5 * v * (1.0 + np.tanh(np.sqrt(2.0 / np.pi) * (v + 0.044715 * v**3)))


def setup_inputs():
    return {"base": bf(np.random.standard_normal((M, S))), "x": bf(np.random.standard_normal((K, N))), "w": bf(1.2 * np.random.standard_normal((E, K, M)) / np.sqrt(K)), "w2": bf(np.random.standard_normal((M, O)) / np.sqrt(2 * M)), "b": f32(0.5 * np.random.standard_normal((O, 1))), "offs": striped(np.random.permutation(S)[:N])}


def reference(base, x, w, w2, b, offs):
    idx = offs[:16].T.reshape(-1)
    z = f64(base).copy()
    for e in range(E):
        z[:, idx[e * Q : (e + 1) * Q]] += f64(w)[e].T @ f64(x)[:, e * Q : (e + 1) * Q]
    y = f64(w2).T @ z
    return gelu_tanh(y + f64(b))

@@ -1,0 +1,81 @@
+import concourse.mybir as mybir
+from concourse.masks import make_identity
+
+BF16, F32, U16 = mybir.dt.bfloat16, mybir.dt.float32, mybir.dt.uint16
+GELU_TANH = mybir.ActivationFunctionType.Gelu_apprx_tanh
+
+P = 128
+S, K, M, N = 512, 128, 384, 256
+E, O = 4, 512
+Q = N // E
+ENTRIES_PER_COLUMN = 16
+QC = Q // ENTRIES_PER_COLUMN
+MB, OB = M // P, O // P
+
+FLOPS = 2 * K * M * N + 2 * M * O * S
+
+
+def tile_rows_thenproj_gelu_kernel(tc, base, x, w, w2, b, offs, out):
+    nc = tc.nc
+    with (
+        tc.tile_pool(name="held", bufs=1) as held,
+        tc.psum_pool(name="psum", bufs=1) as psum,
+    ):
+        base_tile = held.tile([P, MB, S], BF16, name="base_tile")
+        offsets = held.tile([P, N // ENTRIES_PER_COLUMN], U16, name="offsets")
+        x_tile = held.tile([P, N], BF16, name="x_tile")
+        w_tile = held.tile([P, E, M], BF16, name="w_tile")
+        w2_tile = held.tile([P, MB, O], BF16, name="w2_tile")
+        bias = held.tile([P, OB], F32, name="bias")
+        nc.sync.dma_start(base_tile[:], base.rearrange("(a p) s -> p a s", p=P))
+        nc.sync.dma_start(offsets[:], offs)
+        nc.sync.dma_start(x_tile[:], x)
+        nc.sync.dma_start(w_tile[:], w.rearrange("e k m -> k e m"))
+        nc.sync.dma_start(w2_tile[:], w2.rearrange("(a p) o -> p a o", p=P))
+        nc.sync.dma_start(bias[:], b.rearrange("(a p) o -> p (a o)", p=P))
+
+        ident = held.tile([P, P], BF16, name="ident")
+        make_identity(nc, ident[:])
+
+        windows = [psum.tile([P, S], F32, name=f"window{a}") for a in range(MB)]
+        for a in range(MB):
+            nc.tensor.matmul(windows[a][:], ident[:], base_tile[:, a, :], start=True, stop=False)
+
+        for a in range(MB):
+            for e in range(E):
+                nc.tensor.matmul(
+                    windows[a][:].indirect(offsets[:, e * QC : (e + 1) * QC]),
+                    w_tile[:, e, a * P : (a + 1) * P],
+                    x_tile[:, e * Q : (e + 1) * Q],
+                    start=False,
+                    stop=e == E - 1,
+                )
+
+        z_tiles = [held.tile([P, S], BF16, name=f"z{a}") for a in range(MB)]
+        for a in range(MB):
+            if a % 2 == 0:
+                nc.vector.tensor_copy(z_tiles[a][:], windows[a][:])
+            else:
+                nc.scalar.copy(z_tiles[a][:], windows[a][:])
+
+        products = [psum.tile([P, S], F32, name=f"product{c}") for c in range(OB)]
+
+        def project(c, a):
+            nc.tensor.matmul(
+                products[c][:],
+                w2_tile[:, a, c * P : (c + 1) * P],
+                z_tiles[a][:],
+                start=a == 0,
+                stop=a == MB - 1,
+            )
+
+        for c in range(OB):
+            project(c, 0)
+        for c in range(OB):
+            for a in range(1, MB):
+                project(c, a)
+
+        for c in range(OB):
+            result = held.tile([P, S], F32, name=f"result{c}")
+            nc.scalar.activation(result[:], products[c][:], GELU_TANH, bias=bias[:, c : c + 1])
+            nc.sync.dma_start(out[c * P : (c + 1) * P, :], result[:])

@@ -11,6 +11,7 @@ Q = N // E
 ENTRIES_PER_COLUMN = 16
 QC = Q // ENTRIES_PER_COLUMN
 MB, OB = M // P, O // P
+WARM_UPS = 6
 
 FLOPS = 2 * K * M * N + 2 * M * O * S
 
@@ -33,6 +34,12 @@ def tile_rows_thenproj_gelu_kernel(tc, base, x, w, w2, b, offs, out):
         nc.sync.dma_start(w_tile[:], w.rearrange("e k m -> k e m"))
         nc.sync.dma_start(w2_tile[:], w2.rearrange("(a p) o -> p a o", p=P))
         nc.sync.dma_start(bias[:], b.rearrange("(a p) o -> p (a o)", p=P))
+
+        zeros = held.tile([P, S], BF16, name="zeros")
+        nc.vector.memset(zeros[:], 0.0)
+        unread = psum.tile([P, S], F32, name="unread")
+        for warm_up in range(WARM_UPS):
+            nc.tensor.matmul(unread[:], zeros[:, :P], zeros[:], start=True, stop=True)
 
         ident = held.tile([P, P], BF16, name="ident")
         make_identity(nc, ident[:])

@@ -11,7 +11,9 @@ Q = N // E
 ENTRIES_PER_COLUMN = 16
 QC = Q // ENTRIES_PER_COLUMN
 MB, OB = M // P, O // P
-WARM_UPS = 6
+WARM_UPS = 3
+PIECES = [(c, 0, S) for c in range(OB - 1)] + [(OB - 1, 0, S // 2), (OB - 1, S // 2, S // 2)]
+EARLY = 2
 
 FLOPS = 2 * K * M * N + 2 * M * O * S
 
@@ -37,9 +39,12 @@ def tile_rows_thenproj_gelu_kernel(tc, base, x, w, w2, b, offs, out):
 
         zeros = held.tile([P, S], BF16, name="zeros")
         nc.vector.memset(zeros[:], 0.0)
-        unread = psum.tile([P, S], F32, name="unread")
+        products = [psum.tile([P, width], F32, name=f"product{c}_{first}") for c, first, width in PIECES]
         for warm_up in range(WARM_UPS):
-            nc.tensor.matmul(unread[:], zeros[:, :P], zeros[:], start=True, stop=True)
+            nc.tensor.matmul(products[0][:], zeros[:, :P], zeros[:], start=True, stop=True)
+
+        table_trigger = held.tile([P, 1], F32, name="table_trigger")
+        nc.scalar.activation(table_trigger[:], zeros[:, :1], GELU_TANH)
 
         ident = held.tile([P, P], BF16, name="ident")
         make_identity(nc, ident[:])
@@ -65,24 +70,26 @@ def tile_rows_thenproj_gelu_kernel(tc, base, x, w, w2, b, offs, out):
             else:
                 nc.scalar.copy(z_tiles[a][:], windows[a][:])
 
-        products = [psum.tile([P, S], F32, name=f"product{c}") for c in range(OB)]
-
-        def project(c, a):
+        def project(product, piece, a):
+            c, first, width = piece
             nc.tensor.matmul(
-                products[c][:],
+                product[:],
                 w2_tile[:, a, c * P : (c + 1) * P],
-                z_tiles[a][:],
+                z_tiles[a][:, first : first + width],
                 start=a == 0,
                 stop=a == MB - 1,
             )
 
-        for c in range(OB):
-            project(c, 0)
-        for c in range(OB):
-            for a in range(1, MB):
-                project(c, a)
+        for product, piece in list(zip(products, PIECES))[:EARLY]:
+            for a in range(MB - 1):
+                project(product, piece, a)
+        for product, piece in list(zip(products, PIECES))[:EARLY]:
+            project(product, piece, MB - 1)
+        for product, piece in list(zip(products, PIECES))[EARLY:]:
+            for a in range(MB):
+                project(product, piece, a)
 
-        for c in range(OB):
-            result = held.tile([P, S], F32, name=f"result{c}")
-            nc.scalar.activation(result[:], products[c][:], GELU_TANH, bias=bias[:, c : c + 1])
-            nc.sync.dma_start(out[c * P : (c + 1) * P, :], result[:])
+        for product, (c, first, width) in zip(products, PIECES):
+            result = held.tile([P, width], F32, name=f"result{c}_{first}")
+            nc.scalar.activation(result[:], product[:], GELU_TANH, bias=bias[:, c : c + 1])
+            nc.sync.dma_start(out[c * P : (c + 1) * P, first : first + width], result[:])

@@ -11,6 +11,8 @@ Q = N // E
 ENTRIES_PER_COLUMN = 16
 QC = Q // ENTRIES_PER_COLUMN
 MB, OB = M // P, O // P
+SHARES = [(0, P), (P, M - P)]
+
 WARM_UPS = 3
 PIECES = [(c, 0, S) for c in range(OB - 1)] + [(OB - 1, 0, S // 2), (OB - 1, S // 2, S // 2)]
 EARLY = 2
@@ -24,16 +26,19 @@ def tile_rows_thenproj_gelu_kernel(tc, base, x, w, w2, b, offs, out):
         tc.tile_pool(name="held", bufs=1) as held,
         tc.psum_pool(name="psum", bufs=1) as psum,
     ):
-        base_tile = held.tile([P, MB, S], BF16, name="base_tile")
+        base_tiles = [held.tile([P, width // P, S], BF16, name=f"base_tile{first}") for first, width in SHARES]
         offsets = held.tile([P, N // ENTRIES_PER_COLUMN], U16, name="offsets")
         x_tile = held.tile([P, N], BF16, name="x_tile")
-        w_tile = held.tile([P, E, M], BF16, name="w_tile")
+        w_tiles = [held.tile([P, E, width], BF16, name=f"w_tile{first}") for first, width in SHARES]
         w2_tile = held.tile([P, MB, O], BF16, name="w2_tile")
         bias = held.tile([P, OB], F32, name="bias")
-        nc.sync.dma_start(base_tile[:], base.rearrange("(a p) s -> p a s", p=P))
+        for base_tile, (first, width) in zip(base_tiles, SHARES):
+            rows = base[first : first + width, :]
+            nc.sync.dma_start(base_tile[:], rows.rearrange("(a p) s -> p a s", p=P))
         nc.sync.dma_start(offsets[:], offs)
         nc.sync.dma_start(x_tile[:], x)
-        nc.sync.dma_start(w_tile[:], w.rearrange("e k m -> k e m"))
+        for w_tile, (first, width) in zip(w_tiles, SHARES):
+            nc.sync.dma_start(w_tile[:], w[:, :, first : first + width].rearrange("e k m -> k e m"))
         nc.sync.dma_start(w2_tile[:], w2.rearrange("(a p) o -> p a o", p=P))
         nc.sync.dma_start(bias[:], b.rearrange("(a p) o -> p (a o)", p=P))
 
@@ -50,18 +55,22 @@ def tile_rows_thenproj_gelu_kernel(tc, base, x, w, w2, b, offs, out):
         make_identity(nc, ident[:])
 
         windows = [psum.tile([P, S], F32, name=f"window{a}") for a in range(MB)]
-        for a in range(MB):
-            nc.tensor.matmul(windows[a][:], ident[:], base_tile[:, a, :], start=True, stop=False)
+        for base_tile, (first, width) in zip(base_tiles, SHARES):
+            for block in range(width // P):
+                window = windows[first // P + block]
+                nc.tensor.matmul(window[:], ident[:], base_tile[:, block, :], start=True, stop=False)
 
-        for a in range(MB):
-            for e in range(E):
-                nc.tensor.matmul(
-                    windows[a][:].indirect(offsets[:, e * QC : (e + 1) * QC]),
-                    w_tile[:, e, a * P : (a + 1) * P],
-                    x_tile[:, e * Q : (e + 1) * Q],
-                    start=False,
-                    stop=e == E - 1,
-                )
+        for w_tile, (first, width) in zip(w_tiles, SHARES):
+            for block in range(width // P):
+                window = windows[first // P + block]
+                for e in range(E):
+                    nc.tensor.matmul(
+                        window[:].indirect(offsets[:, e * QC : (e + 1) * QC]),
+                        w_tile[:, e, block * P : (block + 1) * P],
+                        x_tile[:, e * Q : (e + 1) * Q],
+                        start=False,
+                        stop=e == E - 1,
+                    )
 
         z_tiles = [held.tile([P, S], BF16, name=f"z{a}") for a in range(MB)]
         for a in range(MB):

import concourse.mybir as mybir
from concourse.masks import make_identity

BF16, F32, U16 = mybir.dt.bfloat16, mybir.dt.float32, mybir.dt.uint16
GELU_TANH = mybir.ActivationFunctionType.Gelu_apprx_tanh

P = 128
S, K, M, N = 512, 128, 384, 256
E, O = 4, 512
Q = N // E
ENTRIES_PER_COLUMN = 16
QC = Q // ENTRIES_PER_COLUMN
MB, OB = M // P, O // P
SHARES = [(0, P), (P, M - P)]

WARM_UPS = 3
PIECES = [(c, 0, S) for c in range(OB - 1)] + [(OB - 1, 0, S // 2), (OB - 1, S // 2, S // 2)]
EARLY = 2

FLOPS = 2 * K * M * N + 2 * M * O * S


def tile_rows_thenproj_gelu_kernel(tc, base, x, w, w2, b, offs, out):
    nc = tc.nc
    with (
        tc.tile_pool(name="held", bufs=1) as held,
        tc.psum_pool(name="psum", bufs=1) as psum,
    ):
        base_tiles = [held.tile([P, width // P, S], BF16, name=f"base_tile{first}") for first, width in SHARES]
        offsets = held.tile([P, N // ENTRIES_PER_COLUMN], U16, name="offsets")
        x_tile = held.tile([P, N], BF16, name="x_tile")
        w_tiles = [held.tile([P, E, width], BF16, name=f"w_tile{first}") for first, width in SHARES]
        w2_tile = held.tile([P, MB, O], BF16, name="w2_tile")
        bias = held.tile([P, OB], F32, name="bias")
        for base_tile, (first, width) in zip(base_tiles, SHARES):
            rows = base[first : first + width, :]
            nc.sync.dma_start(base_tile[:], rows.rearrange("(a p) s -> p a s", p=P))
        nc.sync.dma_start(offsets[:], offs)
        nc.sync.dma_start(x_tile[:], x)
        for w_tile, (first, width) in zip(w_tiles, SHARES):
            nc.sync.dma_start(w_tile[:], w[:, :, first : first + width].rearrange("e k m -> k e m"))
        nc.sync.dma_start(w2_tile[:], w2.rearrange("(a p) o -> p a o", p=P))
        nc.sync.dma_start(bias[:], b.rearrange("(a p) o -> p (a o)", p=P))

        zeros = held.tile([P, S], BF16, name="zeros")
        nc.vector.memset(zeros[:], 0.0)
        products = [psum.tile([P, width], F32, name=f"product{c}_{first}") for c, first, width in PIECES]
        for warm_up in range(WARM_UPS):
            nc.tensor.matmul(products[0][:], zeros[:, :P], zeros[:], start=True, stop=True)

        table_trigger = held.tile([P, 1], F32, name="table_trigger")
        nc.scalar.activation(table_trigger[:], zeros[:, :1], GELU_TANH)

        ident = held.tile([P, P], BF16, name="ident")
        make_identity(nc, ident[:])

        windows = [psum.tile([P, S], F32, name=f"window{a}") for a in range(MB)]
        for base_tile, (first, width) in zip(base_tiles, SHARES):
            for block in range(width // P):
                window = windows[first // P + block]
                nc.tensor.matmul(window[:], ident[:], base_tile[:, block, :], start=True, stop=False)

        for w_tile, (first, width) in zip(w_tiles, SHARES):
            for block in range(width // P):
                window = windows[first // P + block]
                for e in range(E):
                    nc.tensor.matmul(
                        window[:].indirect(offsets[:, e * QC : (e + 1) * QC]),
                        w_tile[:, e, block * P : (block + 1) * P],
                        x_tile[:, e * Q : (e + 1) * Q],
                        start=False,
                        stop=e == E - 1,
                    )

        z_tiles = [held.tile([P, S], BF16, name=f"z{a}") for a in range(MB)]
        for a in range(MB):
            if a % 2 == 0:
                nc.vector.tensor_copy(z_tiles[a][:], windows[a][:])
            else:
                nc.scalar.copy(z_tiles[a][:], windows[a][:])

        def project(product, piece, a):
            c, first, width = piece
            nc.tensor.matmul(
                product[:],
                w2_tile[:, a, c * P : (c + 1) * P],
                z_tiles[a][:, first : first + width],
                start=a == 0,
                stop=a == MB - 1,
            )

        for product, piece in list(zip(products, PIECES))[:EARLY]:
            for a in range(MB - 1):
                project(product, piece, a)
        for product, piece in list(zip(products, PIECES))[:EARLY]:
            project(product, piece, MB - 1)
        for product, piece in list(zip(products, PIECES))[EARLY:]:
            for a in range(MB):
                project(product, piece, a)

        for product, (c, first, width) in zip(products, PIECES):
            result = held.tile([P, width], F32, name=f"result{c}_{first}")
            nc.scalar.activation(result[:], product[:], GELU_TANH, bias=bias[:, c : c + 1])
            nc.sync.dma_start(out[c * P : (c + 1) * P, first : first + width], result[:])
